import numpy as np
import ml_dtypes


def mxq(x, axis, fmt="e4m3"):
    dtype, down = {"e4m3": (ml_dtypes.float8_e4m3fn, 7), "e5m2": (ml_dtypes.float8_e5m2, 14)}[fmt]
    v = np.moveaxis(np.asarray(x, np.float32).astype(ml_dtypes.bfloat16).astype(np.float64), axis, -1)
    blocks = v.reshape(v.shape[:-1] + (-1, 32))
    amax = np.abs(blocks).max(-1, keepdims=True)
    byte = np.maximum(np.where(amax > 0, np.frexp(amax)[1] - 1 + 127, 0) - down, 1)
    scale = np.exp2(byte - 127.0)
    codes = (blocks / scale).astype(np.float32).astype(dtype).astype(np.float64)
    return np.moveaxis((codes * scale).reshape(v.shape), -1, axis)


WIDE = False


def mx_kscale(k):
    if not WIDE:
        return np.ones(k)
    levels = np.array([30, -30])
    if k % 512:
        return np.exp2(np.random.permutation(np.resize(levels, k // 32))).repeat(32)
    a = np.empty((k // 512, 16))
    for p in range(k // 512):
        a[p, :8] = np.random.permutation(np.resize(levels, 8))
        for g in range(8):
            far = levels[np.abs(levels - a[p, g]) >= 10]
            a[p, g + 8] = far[np.random.randint(len(far))]
    return np.exp2(a.ravel()).repeat(32)


def f64(x):
    return np.asarray(x).astype(np.float64)


def striped(idx):
    return np.tile(np.asarray(idx).reshape(-1, 16).T, (8, 1)).astype(np.uint16)


def unstriped(offs):
    return offs[:16].T.reshape(-1).astype(np.int64)


K, T, J, I, V, C = 1024, 1024, 256, 256, 1024, 1024


def setup_inputs():
    n = np.random.standard_normal
    idx = np.random.permutation(T)[:J]
    idx2 = np.random.permutation(V)[:I]
    idx3 = np.random.permutation(C)[:I]
    fk = mx_kscale(K)
    return {
        "xf": (n((K, T)) * 0.03).astype(np.float32),
        "fk": (np.random.uniform(0.5, 2.0, (K, 1)) * fk[:, None]).astype(np.float32),
        "kf": (n((K, V))).astype(np.float32),
        "ko": (n((K, I)) * 0.6).astype(np.float32),
        "fi": (np.random.uniform(0.5, 2.0, (K, 1)) / fk[:, None]).astype(np.float32),
        "bi": (np.random.uniform(-0.7, 0.7, (1, I))).astype(np.float32),
        "old": (1.0 * n((J, C))).astype(np.float32),
        "offs": striped(idx),
        "offs2": striped(idx2),
        "offs3": striped(idx3),
    }


def reference(xf, fk, kf, ko, fi, bi, old, offs, offs2, offs3):
    idx = unstriped(offs)
    idx2 = unstriped(offs2)
    idx3 = unstriped(offs3)
    xg = f64(xf)[:, idx]
    x1 = np.pad(xg, ((0, 0), (1, 0)))[:, :J]
    u = (xg - 0.6 * x1) * f64(fk)
    vk = (f64(kf)[:, idx2] + f64(ko)) * f64(fi)
    uq = mxq(u, 0, "e5m2")
    vkq = mxq(vk, 0, "e5m2")
    a0 = uq.T @ vkq
    a = a0 + f64(bi)
    pp = np.zeros((J, C))
    pp[:, idx3] = a
    y = np.maximum(pp, f64(old))
    return y

@@ -1,0 +1,177 @@
+from contextlib import ExitStack
+
+import concourse.mybir as mybir
+from concourse.masks import make_identity
+
+K, T, J, I, V, C = 1024, 1024, 256, 256, 1024, 1024
+FLOPS = 2 * K * J * I
+
+F32 = mybir.dt.float32
+BF16 = mybir.dt.bfloat16
+U32 = mybir.dt.uint32
+U16 = mybir.dt.uint16
+U8 = mybir.dt.uint8
+E5M2X4 = mybir.dt.float8_e5m2_x4
+MULT = mybir.AluOpType.mult
+ADD = mybir.AluOpType.add
+MAX = mybir.AluOpType.max
+COPY = mybir.ActivationFunctionType.Copy
+
+P = 128
+PACK = 4
+PASSES = K // (P * PACK)
+PAD = 8
+STEP = 0.6
+LIST_COLS = J // 16
+HALF_COLS = LIST_COLS // 2
+
+
+def pass_rows(src, a):
+    return src[a * P * PACK : (a + 1) * P * PACK, :].rearrange("(p t) w -> p t w", t=PACK)
+
+
+def tile_list_scores_steps_mixed_placed_f_kernel(tc, xf, fk, kf, ko, fi, bi, old, offs, offs2, offs3, out):
+    nc = tc.nc
+    with ExitStack() as ctx:
+        pool = ctx.enter_context(tc.tile_pool(name="pool", bufs=1))
+        psum = ctx.enter_context(tc.psum_pool(name="psum", bufs=1))
+
+        tok_list = pool.tile([P, LIST_COLS], U16, name="tok_list")
+        key_list = pool.tile([P, LIST_COLS], U16, name="key_list")
+        col_list = pool.tile([P, LIST_COLS], U16, name="col_list")
+        fk_sb = pool.tile([P, PASSES, PACK], F32, name="fk_sb")
+        fi_sb = pool.tile([P, PASSES, PACK], F32, name="fi_sb")
+        bi_sb = pool.tile([P, 2], F32, name="bi_sb")
+        x0 = pool.tile([P, PACK, T], F32, name="x0")
+        k0 = pool.tile([P, PACK, V], F32, name="k0")
+        k1 = [pool.tile([P, 2, V], F32, name=f"k1_{n}") for n in range(2)]
+        x1 = [pool.tile([P, T], F32, name=f"x1_{t}") for t in range(PACK)]
+        ko_sb = pool.tile([P, PASSES, PACK * I], F32, name="ko_sb")
+        old_sb = [pool.tile([P, C], F32, name=f"old_{h}") for h in range(2)]
+
+        nc.sync.dma_start(x0[:], pass_rows(xf, 0))
+        nc.scalar.dma_start(fk_sb[:], fk.rearrange("(a p t) o -> p a (t o)", a=PASSES, t=PACK))
+        nc.scalar.dma_start(fi_sb[:], fi.rearrange("(a p t) o -> p a (t o)", a=PASSES, t=PACK))
+        nc.scalar.dma_start(bi_sb[:], bi.rearrange("o (p m) -> p (o m)", m=2))
+        nc.sync.dma_start(tok_list[:], offs)
+        nc.sync.dma_start(ko_sb[:], ko.rearrange("(a p t) i -> p a (t i)", a=PASSES, t=PACK))
+        nc.sync.dma_start(key_list[:], offs2)
+        nc.sync.dma_start(k0[:], pass_rows(kf, 0))
+        for n in range(2):
+            nc.sync.dma_start(k1[n][:], pass_rows(kf, 1)[:, 2 * n : 2 * n + 2, :])
+        nc.sync.dma_start(col_list[:], offs3)
+        for t in range(PACK):
+            nc.sync.dma_start(x1[t][:], pass_rows(xf, 1)[:, t, :])
+        for h in range(2):
+            nc.sync.dma_start(old_sb[h][:], old[h * P : (h + 1) * P, :])
+
+        ident = pool.tile([P, P], F32, name="ident")
+        make_identity(nc, ident[:])
+        xg = [pool.tile([P, PACK, PAD + J], F32, name=f"xg_{a}") for a in range(PASSES)]
+        for a in range(PASSES):
+            nc.gpsimd.memset(xg[a][:, :, 0:PAD], 0.0)
+        board = [pool.tile([P, C], F32, name=f"board_{h}") for h in range(2)]
+        for h in range(2):
+            nc.gpsimd.memset(board[h][:], 0.0)
+
+        bias_ps = psum.tile([P, 2, P], F32, name="bias_ps")
+        for m in range(2):
+            nc.tensor.transpose(bias_ps[:, m, :], bi_sb[:, m : m + 1].to_broadcast([P, P]), ident[:])
+        bias = pool.tile([P, I], F32, name="bias")
+        nc.scalar.activation(bias[:].rearrange("p (n m) -> p n m", m=2), bias_ps[:].rearrange("p m n -> p n m"), COPY)
+
+        def quantise(name, grouped, width):
+            codes = pool.tile([P, width], U32, name=name + "_codes", align_bytes=64)
+            scales = pool.tile([P, width], U8, name=name + "_scales", align_bytes=64)
+            nc.vector.quantize_mx(codes[:].bitcast(E5M2X4), scales[:], grouped[:].rearrange("p w t -> p (w t)"))
+            return codes, scales
+
+        def interleave(name, planes):
+            grouped = pool.tile([P, J, PACK], BF16, name=name + "_grouped", align_bytes=64)
+            nc.vector.tensor_copy(
+                grouped[:].rearrange("p (c i) t -> p c t i", i=4),
+                planes[:].rearrange("p t (c i) -> p c t i", i=4),
+            )
+            return grouped
+
+        diff0 = pool.tile([P, PACK, J], F32, name="diff0")
+        u0 = pool.tile([P, PACK, J], BF16, name="u0")
+        for t in range(PACK):
+            nc.scalar.activation(xg[0][:, t, PAD:], x0[:, t, :].indirect(tok_list[:]), COPY)
+        for t in range(PACK):
+            nc.vector.scalar_tensor_tensor(
+                diff0[:, t, :], xg[0][:, t, PAD - 1 : PAD - 1 + J], -STEP, xg[0][:, t, PAD:], MULT, ADD
+            )
+        for t in range(PACK):
+            nc.vector.tensor_scalar(u0[:, t, :], diff0[:, t, :], fk_sb[:, 0, t : t + 1], None, MULT)
+        u0_codes, u0_scales = quantise("u0", interleave("u0", u0), J)
+
+        kos = pool.tile([P, PASSES, PACK * I], F32, name="kos")
+        for a in range(PASSES):
+            for t in range(PACK):
+                cols = slice(t * I, (t + 1) * I)
+                nc.scalar.activation(kos[:, a, cols], ko_sb[:, a, cols], COPY, scale=fi_sb[:, a, t : t + 1])
+
+        def keys(a, windows):
+            kg = pool.tile([P, PACK, I], F32, name=f"kg_{a}")
+            vk = pool.tile([P, PACK, I], BF16, name=f"vk_{a}")
+            for t in range(PACK):
+                nc.scalar.activation(kg[:, t, :], windows[t].indirect(key_list[:]), COPY)
+                nc.vector.scalar_tensor_tensor(
+                    vk[:, t, :], kg[:, t, :], fi_sb[:, a, t : t + 1], kos[:, a, t * I : (t + 1) * I], MULT, ADD
+                )
+            return quantise(f"vk_{a}", interleave(f"vk_{a}", vk), I)
+
+        acc = [psum.tile([P, I], F32, name=f"acc_{h}") for h in range(2)]
+        v0_codes, v0_scales = keys(0, [k0[:, t, :] for t in range(PACK)])
+        for h in range(2):
+            rows = slice(h * P, (h + 1) * P)
+            nc.tensor.matmul_mx(
+                acc[h][:], u0_codes[:, rows].bitcast(E5M2X4), u0_scales[:, rows],
+                v0_codes[:].bitcast(E5M2X4), v0_scales[:], start=True, stop=False,
+            )
+        v1_codes, v1_scales = keys(1, [k1[t // 2][:, t % 2, :] for t in range(PACK)])
+
+        diff1 = pool.tile([P, PACK, J], F32, name="diff1")
+        u1 = [pool.tile([P, P, PACK], BF16, name=f"u1_{h}", align_bytes=64) for h in range(2)]
+        last = PACK - 1
+        for t in range(last):
+            nc.scalar.activation(xg[1][:, t, PAD:], x1[t][:].indirect(tok_list[:]), COPY)
+            nc.vector.scalar_tensor_tensor(
+                diff1[:, t, :], xg[1][:, t, PAD - 1 : PAD - 1 + J], -STEP, xg[1][:, t, PAD:], MULT, ADD
+            )
+            for h in range(2):
+                nc.vector.tensor_scalar(
+                    u1[h][:, :, t], diff1[:, t, h * P : (h + 1) * P], fk_sb[:, 1, t : t + 1], None, MULT
+                )
+        nc.vector.tensor_copy(xg[1][:, last, PAD : PAD + P], x1[last][:].indirect(tok_list[:, 0:HALF_COLS]))
+        nc.scalar.activation(xg[1][:, last, PAD + P :], x1[last][:].indirect(tok_list[:, HALF_COLS:]), COPY)
+        for h in range(2):
+            lo = PAD + h * P
+            nc.vector.scalar_tensor_tensor(
+                diff1[:, last, h * P : (h + 1) * P], xg[1][:, last, lo - 1 : lo - 1 + P], -STEP,
+                xg[1][:, last, lo : lo + P], MULT, ADD,
+            )
+        for h in range(2):
+            nc.vector.tensor_scalar(
+                u1[h][:, :, last], diff1[:, last, h * P : (h + 1) * P], fk_sb[:, 1, last : last + 1], None, MULT
+            )
+        for h in range(2):
+            codes, scales = quantise(f"u1_{h}", u1[h], P)
+            nc.tensor.matmul_mx(
+                acc[h][:], codes[:].bitcast(E5M2X4), scales[:],
+                v1_codes[:].bitcast(E5M2X4), v1_scales[:], start=False, stop=True,
+            )
+
+        scores = [pool.tile([P, I], F32, name=f"scores_{h}") for h in range(2)]
+        for h in range(2):
+            nc.vector.tensor_tensor(scores[h][:], acc[h][:], bias[:], ADD)
+        nc.scalar.activation(board[0][:].indirect(col_list[:]), scores[0][:], COPY)
+        nc.vector.tensor_copy(board[1][:].indirect(col_list[:, 0:HALF_COLS]), scores[1][:, 0:P])
+        nc.scalar.activation(board[1][:].indirect(col_list[:, HALF_COLS:]), scores[1][:, P:], COPY)
+
+        pieces = [(0, 0, 512), (0, 512, 1024), (1, 0, 512), (1, 512, 768), (1, 768, 1024)]
+        for h, lo, hi in pieces:
+            best = pool.tile([P, hi - lo], F32, name=f"best_{h}_{lo}")
+            nc.vector.tensor_tensor(best[:], board[h][:, lo:hi], old_sb[h][:, lo:hi], MAX)
+            nc.sync.dma_start(out[h * P : (h + 1) * P, lo:hi], best[:])

@@ -42,34 +42,34 @@ def tile_list_scores_steps_mixed_placed_f_kernel(tc, xf, fk, kf, ko, fi, bi, old
         fk_sb = pool.tile([P, PASSES, PACK], F32, name="fk_sb")
         fi_sb = pool.tile([P, PASSES, PACK], F32, name="fi_sb")
         bi_sb = pool.tile([P, 2], F32, name="bi_sb")
-        x0 = pool.tile([P, PACK, T], F32, name="x0")
-        k0 = pool.tile([P, PACK, V], F32, name="k0")
-        k1 = [pool.tile([P, 2, V], F32, name=f"k1_{n}") for n in range(2)]
-        x1 = [pool.tile([P, T], F32, name=f"x1_{t}") for t in range(PACK)]
         ko_sb = pool.tile([P, PASSES, PACK * I], F32, name="ko_sb")
         old_sb = [pool.tile([P, C], F32, name=f"old_{h}") for h in range(2)]
 
-        nc.sync.dma_start(x0[:], pass_rows(xf, 0))
-        nc.scalar.dma_start(fk_sb[:], fk.rearrange("(a p t) o -> p a (t o)", a=PASSES, t=PACK))
+        def load_planes(name, src, a, first, count):
+            planes = pool.tile([P, count, src.shape[1]], F32, name=f"{name}_{a}_{first}")
+            nc.sync.dma_start(planes[:], pass_rows(src, a)[:, first : first + count, :])
+            return [planes[:, e, :] for e in range(count)]
+
         nc.scalar.dma_start(fi_sb[:], fi.rearrange("(a p t) o -> p a (t o)", a=PASSES, t=PACK))
+        nc.sync.dma_start(ko_sb[:], ko.rearrange("(a p t) i -> p a (t i)", a=PASSES, t=PACK))
+        nc.scalar.dma_start(fk_sb[:], fk.rearrange("(a p t) o -> p a (t o)", a=PASSES, t=PACK))
         nc.scalar.dma_start(bi_sb[:], bi.rearrange("o (p m) -> p (o m)", m=2))
         nc.sync.dma_start(tok_list[:], offs)
-        nc.sync.dma_start(ko_sb[:], ko.rearrange("(a p t) i -> p a (t i)", a=PASSES, t=PACK))
+        x0 = load_planes("x", xf, 0, 0, 2) + load_planes("x", xf, 0, 2, 2)
         nc.sync.dma_start(key_list[:], offs2)
-        nc.sync.dma_start(k0[:], pass_rows(kf, 0))
-        for n in range(2):
-            nc.sync.dma_start(k1[n][:], pass_rows(kf, 1)[:, 2 * n : 2 * n + 2, :])
+        k0 = load_planes("k", kf, 0, 0, 2) + load_planes("k", kf, 0, 2, 2)
+        x1 = load_planes("x", xf, 1, 0, 2) + load_planes("x", xf, 1, 2, 1) + load_planes("x", xf, 1, 3, 1)
+        k1 = [load_planes("k", kf, 1, t, 1)[0] for t in range(PACK)]
         nc.sync.dma_start(col_list[:], offs3)
-        for t in range(PACK):
-            nc.sync.dma_start(x1[t][:], pass_rows(xf, 1)[:, t, :])
         for h in range(2):
             nc.sync.dma_start(old_sb[h][:], old[h * P : (h + 1) * P, :])
 
         ident = pool.tile([P, P], F32, name="ident")
         make_identity(nc, ident[:])
-        xg = [pool.tile([P, PACK, PAD + J], F32, name=f"xg_{a}") for a in range(PASSES)]
+        xg = [[pool.tile([P, PAD + J], F32, name=f"xg_{a}_{t}") for t in range(PACK)] for a in range(PASSES)]
         for a in range(PASSES):
-            nc.gpsimd.memset(xg[a][:, :, 0:PAD], 0.0)
+            for t in range(PACK):
+                nc.gpsimd.memset(xg[a][t][:, 0:PAD], 0.0)
         board = [pool.tile([P, C], F32, name=f"board_{h}") for h in range(2)]
         for h in range(2):
             nc.gpsimd.memset(board[h][:], 0.0)
@@ -86,89 +86,81 @@ def tile_list_scores_steps_mixed_placed_f_kernel(tc, xf, fk, kf, ko, fi, bi, old
             nc.vector.quantize_mx(codes[:].bitcast(E5M2X4), scales[:], grouped[:].rearrange("p w t -> p (w t)"))
             return codes, scales
 
-        def interleave(name, planes):
-            grouped = pool.tile([P, J, PACK], BF16, name=name + "_grouped", align_bytes=64)
-            nc.vector.tensor_copy(
-                grouped[:].rearrange("p (c i) t -> p c t i", i=4),
-                planes[:].rearrange("p t (c i) -> p c t i", i=4),
-            )
-            return grouped
-
-        diff0 = pool.tile([P, PACK, J], F32, name="diff0")
-        u0 = pool.tile([P, PACK, J], BF16, name="u0")
-        for t in range(PACK):
-            nc.scalar.activation(xg[0][:, t, PAD:], x0[:, t, :].indirect(tok_list[:]), COPY)
-        for t in range(PACK):
-            nc.vector.scalar_tensor_tensor(
-                diff0[:, t, :], xg[0][:, t, PAD - 1 : PAD - 1 + J], -STEP, xg[0][:, t, PAD:], MULT, ADD
-            )
-        for t in range(PACK):
-            nc.vector.tensor_scalar(u0[:, t, :], diff0[:, t, :], fk_sb[:, 0, t : t + 1], None, MULT)
-        u0_codes, u0_scales = quantise("u0", interleave("u0", u0), J)
-
-        kos = pool.tile([P, PASSES, PACK * I], F32, name="kos")
+        kos = [[pool.tile([P, I], F32, name=f"kos_{a}_{t}") for t in range(PACK)] for a in range(PASSES)]
         for a in range(PASSES):
             for t in range(PACK):
-                cols = slice(t * I, (t + 1) * I)
-                nc.scalar.activation(kos[:, a, cols], ko_sb[:, a, cols], COPY, scale=fi_sb[:, a, t : t + 1])
+                nc.scalar.activation(kos[a][t][:], ko_sb[:, a, t * I : (t + 1) * I], COPY, scale=fi_sb[:, a, t : t + 1])
 
-        def keys(a, windows):
-            kg = pool.tile([P, PACK, I], F32, name=f"kg_{a}")
-            vk = pool.tile([P, PACK, I], BF16, name=f"vk_{a}")
+        def tokens(a, windows):
+            grouped = pool.tile([P, J, PACK], BF16, name=f"u_{a}", align_bytes=64)
             for t in range(PACK):
-                nc.scalar.activation(kg[:, t, :], windows[t].indirect(key_list[:]), COPY)
+                picked = windows[t].indirect(tok_list[:])
+                if a == 0 and t < 2:
+                    nc.vector.tensor_copy(xg[a][t][:, PAD:], picked)
+                else:
+                    nc.scalar.activation(xg[a][t][:, PAD:], picked, COPY)
+                diff = pool.tile([P, J], F32, name=f"diff_{a}_{t}")
                 nc.vector.scalar_tensor_tensor(
-                    vk[:, t, :], kg[:, t, :], fi_sb[:, a, t : t + 1], kos[:, a, t * I : (t + 1) * I], MULT, ADD
+                    diff[:], xg[a][t][:, PAD - 1 : PAD - 1 + J], -STEP, xg[a][t][:, PAD:], MULT, ADD
                 )
-            return quantise(f"vk_{a}", interleave(f"vk_{a}", vk), I)
+                nc.vector.tensor_scalar(grouped[:, :, t], diff[:], fk_sb[:, a, t : t + 1], None, MULT)
+            return quantise(f"u_{a}", grouped, J)
 
-        acc = [psum.tile([P, I], F32, name=f"acc_{h}") for h in range(2)]
-        v0_codes, v0_scales = keys(0, [k0[:, t, :] for t in range(PACK)])
-        for h in range(2):
+        def key_pair(a, n, windows, targets):
+            vk = pool.tile([P, 2, I], BF16, name=f"vk_pair_{a}_{n}")
+            for e in range(2):
+                t = 2 * n + e
+                kg = pool.tile([P, I], F32, name=f"kg_{a}_{t}")
+                nc.scalar.activation(kg[:], windows[t].indirect(key_list[:]), COPY)
+                nc.vector.scalar_tensor_tensor(vk[:, e, :], kg[:], fi_sb[:, a, t : t + 1], kos[a][t][:], MULT, ADD)
+            for lo, hi, grouped in targets:
+                nc.vector.tensor_copy(
+                    grouped[:, :, 2 * n : 2 * n + 2].rearrange("p (c i) e -> p c e i", i=4),
+                    vk[:, :, lo:hi].rearrange("p e (c i) -> p c e i", i=4),
+                )
+
+        def multiply(acc, u, h, v, start, stop):
             rows = slice(h * P, (h + 1) * P)
             nc.tensor.matmul_mx(
-                acc[h][:], u0_codes[:, rows].bitcast(E5M2X4), u0_scales[:, rows],
-                v0_codes[:].bitcast(E5M2X4), v0_scales[:], start=True, stop=False,
+                acc, u[0][:, rows].bitcast(E5M2X4), u[1][:, rows], v[0].bitcast(E5M2X4), v[1], start=start, stop=stop
             )
-        v1_codes, v1_scales = keys(1, [k1[t // 2][:, t % 2, :] for t in range(PACK)])
 
-        diff1 = pool.tile([P, PACK, J], F32, name="diff1")
-        u1 = [pool.tile([P, P, PACK], BF16, name=f"u1_{h}", align_bytes=64) for h in range(2)]
-        last = PACK - 1
-        for t in range(last):
-            nc.scalar.activation(xg[1][:, t, PAD:], x1[t][:].indirect(tok_list[:]), COPY)
-            nc.vector.scalar_tensor_tensor(
-                diff1[:, t, :], xg[1][:, t, PAD - 1 : PAD - 1 + J], -STEP, xg[1][:, t, PAD:], MULT, ADD
-            )
-            for h in range(2):
-                nc.vector.tensor_scalar(
-                    u1[h][:, :, t], diff1[:, t, h * P : (h + 1) * P], fk_sb[:, 1, t : t + 1], None, MULT
+        u0 = tokens(0, x0)
+        vk0 = pool.tile([P, I, PACK], BF16, name="vk_0", align_bytes=64)
+        for n in range(2):
+            key_pair(0, n, k0, [(0, I, vk0)])
+        v0 = quantise("vk_0", vk0, I)
+        acc_top = [psum.tile([P, P], F32, name=f"acc_top_{g}") for g in range(2)]
+        acc_low = psum.tile([P, I], F32, name="acc_low")
+        for g in range(2):
+            cols = slice(g * P, (g + 1) * P)
+            multiply(acc_top[g][:], u0, 0, (v0[0][:, cols], v0[1][:, cols]), True, False)
+        multiply(acc_low[:], u0, 1, (v0[0][:], v0[1][:]), True, False)
+
+        u1 = tokens(1, x1)
+        vk1 = [pool.tile([P, P, PACK], BF16, name=f"vk_1_{g}", align_bytes=64) for g in range(2)]
+        key_pair(1, 0, k1, [(g * P, (g + 1) * P, vk1[g]) for g in range(2)])
+        for t in range(2, PACK):
+            for g in range(2):
+                cols = slice(g * P, (g + 1) * P)
+                kg = pool.tile([P, P], F32, name=f"kg_half_{t}_{g}")
+                nc.scalar.activation(kg[:], k1[t].indirect(key_list[:, g * HALF_COLS : (g + 1) * HALF_COLS]), COPY)
+                nc.vector.scalar_tensor_tensor(
+                    vk1[g][:, :, t], kg[:], fi_sb[:, 1, t : t + 1], kos[1][t][:, cols], MULT, ADD
                 )
-        nc.vector.tensor_copy(xg[1][:, last, PAD : PAD + P], x1[last][:].indirect(tok_list[:, 0:HALF_COLS]))
-        nc.scalar.activation(xg[1][:, last, PAD + P :], x1[last][:].indirect(tok_list[:, HALF_COLS:]), COPY)
-        for h in range(2):
-            lo = PAD + h * P
-            nc.vector.scalar_tensor_tensor(
-                diff1[:, last, h * P : (h + 1) * P], xg[1][:, last, lo - 1 : lo - 1 + P], -STEP,
-                xg[1][:, last, lo : lo + P], MULT, ADD,
-            )
-        for h in range(2):
-            nc.vector.tensor_scalar(
-                u1[h][:, :, last], diff1[:, last, h * P : (h + 1) * P], fk_sb[:, 1, last : last + 1], None, MULT
-            )
-        for h in range(2):
-            codes, scales = quantise(f"u1_{h}", u1[h], P)
-            nc.tensor.matmul_mx(
-                acc[h][:], codes[:].bitcast(E5M2X4), scales[:],
-                v1_codes[:].bitcast(E5M2X4), v1_scales[:], start=False, stop=True,
-            )
+                if t == PACK - 1:
+                    codes, scales = quantise(f"vk_1_{g}", vk1[g], P)
+                    multiply(acc_top[g][:], u1, 0, (codes[:], scales[:]), False, True)
+                    multiply(acc_low[:, cols], u1, 1, (codes[:], scales[:]), False, g == 1)
 
-        scores = [pool.tile([P, I], F32, name=f"scores_{h}") for h in range(2)]
-        for h in range(2):
-            nc.vector.tensor_tensor(scores[h][:], acc[h][:], bias[:], ADD)
-        nc.scalar.activation(board[0][:].indirect(col_list[:]), scores[0][:], COPY)
-        nc.vector.tensor_copy(board[1][:].indirect(col_list[:, 0:HALF_COLS]), scores[1][:, 0:P])
-        nc.scalar.activation(board[1][:].indirect(col_list[:, HALF_COLS:]), scores[1][:, P:], COPY)
+        top = [pool.tile([P, P], F32, name=f"top_{g}") for g in range(2)]
+        low = pool.tile([P, I], F32, name="low")
+        for g in range(2):
+            nc.scalar.activation(top[g][:], acc_top[g][:], COPY)
+        nc.vector.tensor_tensor(board[0][:].indirect(col_list[:, 0:HALF_COLS]), top[0][:], bias[:, 0:P], ADD)
+        nc.vector.tensor_tensor(low[:], acc_low[:], bias[:], ADD)
+        nc.vector.tensor_tensor(board[0][:].indirect(col_list[:, HALF_COLS:]), top[1][:], bias[:, P:], ADD)
+        nc.scalar.activation(board[1][:].indirect(col_list[:]), low[:], COPY)
 
         pieces = [(0, 0, 512), (0, 512, 1024), (1, 0, 512), (1, 512, 768), (1, 768, 1024)]
         for h, lo, hi in pieces:

@@ -39,8 +39,8 @@ def tile_list_scores_steps_mixed_placed_f_kernel(tc, xf, fk, kf, ko, fi, bi, old
         tok_list = pool.tile([P, LIST_COLS], U16, name="tok_list")
         key_list = pool.tile([P, LIST_COLS], U16, name="key_list")
         col_list = pool.tile([P, LIST_COLS], U16, name="col_list")
-        fk_sb = pool.tile([P, PASSES, PACK], F32, name="fk_sb")
-        fi_sb = pool.tile([P, PASSES, PACK], F32, name="fi_sb")
+        fk_sb = pool.tile([P, PASSES, PAD], F32, name="fk_sb")
+        fi_sb = pool.tile([P, PASSES, PAD], F32, name="fi_sb")
         bi_sb = pool.tile([P, 2], F32, name="bi_sb")
         ko_sb = pool.tile([P, PASSES, PACK * I], F32, name="ko_sb")
         old_sb = [pool.tile([P, C], F32, name=f"old_{h}") for h in range(2)]
@@ -50,12 +50,12 @@ def tile_list_scores_steps_mixed_placed_f_kernel(tc, xf, fk, kf, ko, fi, bi, old
             nc.sync.dma_start(planes[:], pass_rows(src, a)[:, first : first + count, :])
             return [planes[:, e, :] for e in range(count)]
 
-        nc.scalar.dma_start(fi_sb[:], fi.rearrange("(a p t) o -> p a (t o)", a=PASSES, t=PACK))
+        nc.scalar.dma_start(fi_sb[:, :, 0:PACK], fi.rearrange("(a p t) o -> p a (t o)", a=PASSES, t=PACK))
         nc.sync.dma_start(ko_sb[:], ko.rearrange("(a p t) i -> p a (t i)", a=PASSES, t=PACK))
-        nc.scalar.dma_start(fk_sb[:], fk.rearrange("(a p t) o -> p a (t o)", a=PASSES, t=PACK))
+        nc.scalar.dma_start(fk_sb[:, :, 0:PACK], fk.rearrange("(a p t) o -> p a (t o)", a=PASSES, t=PACK))
         nc.scalar.dma_start(bi_sb[:], bi.rearrange("o (p m) -> p (o m)", m=2))
         nc.sync.dma_start(tok_list[:], offs)
-        x0 = load_planes("x", xf, 0, 0, 2) + load_planes("x", xf, 0, 2, 2)
+        x0 = load_planes("x", xf, 0, 0, PACK)
         nc.sync.dma_start(key_list[:], offs2)
         k0 = load_planes("k", kf, 0, 0, 2) + load_planes("k", kf, 0, 2, 2)
         x1 = load_planes("x", xf, 1, 0, 2) + load_planes("x", xf, 1, 2, 1) + load_planes("x", xf, 1, 3, 1)
@@ -64,12 +64,14 @@ def tile_list_scores_steps_mixed_placed_f_kernel(tc, xf, fk, kf, ko, fi, bi, old
         for h in range(2):
             nc.sync.dma_start(old_sb[h][:], old[h * P : (h + 1) * P, :])
 
+        zeros = pool.tile([P, PAD], F32, name="zeros")
+        nc.gpsimd.memset(zeros[:], 0.0)
         ident = pool.tile([P, P], F32, name="ident")
         make_identity(nc, ident[:])
         xg = [[pool.tile([P, PAD + J], F32, name=f"xg_{a}_{t}") for t in range(PACK)] for a in range(PASSES)]
         for a in range(PASSES):
             for t in range(PACK):
-                nc.gpsimd.memset(xg[a][t][:, 0:PAD], 0.0)
+                nc.scalar.activation(xg[a][t][:, 0:PAD], zeros[:], COPY)
         board = [pool.tile([P, C], F32, name=f"board_{h}") for h in range(2)]
         for h in range(2):
             nc.gpsimd.memset(board[h][:], 0.0)
@@ -89,35 +91,37 @@ def tile_list_scores_steps_mixed_placed_f_kernel(tc, xf, fk, kf, ko, fi, bi, old
         kos = [[pool.tile([P, I], F32, name=f"kos_{a}_{t}") for t in range(PACK)] for a in range(PASSES)]
         for a in range(PASSES):
             for t in range(PACK):
-                nc.scalar.activation(kos[a][t][:], ko_sb[:, a, t * I : (t + 1) * I], COPY, scale=fi_sb[:, a, t : t + 1])
+                nc.gpsimd.tensor_scalar(
+                    kos[a][t][:], ko_sb[:, a, t * I : (t + 1) * I], fi_sb[:, a, t : t + 1], 0.0, MULT, ADD
+                )
 
-        def tokens(a, windows):
-            grouped = pool.tile([P, J, PACK], BF16, name=f"u_{a}", align_bytes=64)
-            for t in range(PACK):
-                picked = windows[t].indirect(tok_list[:])
-                if a == 0 and t < 2:
-                    nc.vector.tensor_copy(xg[a][t][:, PAD:], picked)
-                else:
-                    nc.scalar.activation(xg[a][t][:, PAD:], picked, COPY)
+        def weave(grouped, planes, first):
+            count = planes.shape[1]
+            nc.vector.tensor_copy(
+                grouped[:, :, first : first + count].rearrange("p (c i) e -> p c e i", i=4),
+                planes.rearrange("p e (c i) -> p c e i", i=4),
+            )
+
+        def token_planes(a, first, count, windows):
+            planes = pool.tile([P, count, J], BF16, name=f"u_planes_{a}_{first}")
+            for e in range(count):
+                t = first + e
+                nc.scalar.activation(xg[a][t][:, PAD:], windows[t].indirect(tok_list[:]), COPY)
                 diff = pool.tile([P, J], F32, name=f"diff_{a}_{t}")
                 nc.vector.scalar_tensor_tensor(
                     diff[:], xg[a][t][:, PAD - 1 : PAD - 1 + J], -STEP, xg[a][t][:, PAD:], MULT, ADD
                 )
-                nc.vector.tensor_scalar(grouped[:, :, t], diff[:], fk_sb[:, a, t : t + 1], None, MULT)
-            return quantise(f"u_{a}", grouped, J)
+                nc.vector.tensor_scalar(planes[:, e, :], diff[:], fk_sb[:, a, t : t + 1], None, MULT)
+            return planes
 
-        def key_pair(a, n, windows, targets):
-            vk = pool.tile([P, 2, I], BF16, name=f"vk_pair_{a}_{n}")
-            for e in range(2):
-                t = 2 * n + e
+        def key_planes(a, first, count, windows):
+            planes = pool.tile([P, count, I], BF16, name=f"vk_planes_{a}_{first}")
+            for e in range(count):
+                t = first + e
                 kg = pool.tile([P, I], F32, name=f"kg_{a}_{t}")
                 nc.scalar.activation(kg[:], windows[t].indirect(key_list[:]), COPY)
-                nc.vector.scalar_tensor_tensor(vk[:, e, :], kg[:], fi_sb[:, a, t : t + 1], kos[a][t][:], MULT, ADD)
-            for lo, hi, grouped in targets:
-                nc.vector.tensor_copy(
-                    grouped[:, :, 2 * n : 2 * n + 2].rearrange("p (c i) e -> p c e i", i=4),
-                    vk[:, :, lo:hi].rearrange("p e (c i) -> p c e i", i=4),
-                )
+                nc.vector.scalar_tensor_tensor(planes[:, e, :], kg[:], fi_sb[:, a, t : t + 1], kos[a][t][:], MULT, ADD)
+            return planes
 
         def multiply(acc, u, h, v, start, stop):
             rows = slice(h * P, (h + 1) * P)
@@ -125,10 +129,11 @@ def tile_list_scores_steps_mixed_placed_f_kernel(tc, xf, fk, kf, ko, fi, bi, old
                 acc, u[0][:, rows].bitcast(E5M2X4), u[1][:, rows], v[0].bitcast(E5M2X4), v[1], start=start, stop=stop
             )
 
-        u0 = tokens(0, x0)
+        ug0 = pool.tile([P, J, PACK], BF16, name="u_0", align_bytes=64)
+        weave(ug0, token_planes(0, 0, PACK, x0)[:], 0)
+        u0 = quantise("u_0", ug0, J)
         vk0 = pool.tile([P, I, PACK], BF16, name="vk_0", align_bytes=64)
-        for n in range(2):
-            key_pair(0, n, k0, [(0, I, vk0)])
+        weave(vk0, key_planes(0, 0, PACK, k0)[:], 0)
         v0 = quantise("vk_0", vk0, I)
         acc_top = [psum.tile([P, P], F32, name=f"acc_top_{g}") for g in range(2)]
         acc_low = psum.tile([P, I], F32, name="acc_low")
@@ -137,32 +142,57 @@ def tile_list_scores_steps_mixed_placed_f_kernel(tc, xf, fk, kf, ko, fi, bi, old
             multiply(acc_top[g][:], u0, 0, (v0[0][:, cols], v0[1][:, cols]), True, False)
         multiply(acc_low[:], u0, 1, (v0[0][:], v0[1][:]), True, False)
 
-        u1 = tokens(1, x1)
-        vk1 = [pool.tile([P, P, PACK], BF16, name=f"vk_1_{g}", align_bytes=64) for g in range(2)]
-        key_pair(1, 0, k1, [(g * P, (g + 1) * P, vk1[g]) for g in range(2)])
-        for t in range(2, PACK):
+        ug1 = pool.tile([P, J, PACK], BF16, name="u_1", align_bytes=64)
+        for first in (0, 2):
+            weave(ug1, token_planes(1, first, 2, x1)[:], first)
+        u1 = quantise("u_1", ug1, J)
+        early = [pool.tile([P, PACK - 1 + g, P], BF16, name=f"early_{g}") for g in range(2)]
+        for t in range(2):
+            kg = pool.tile([P, I], F32, name=f"kg_1_{t}")
+            nc.scalar.activation(kg[:], k1[t].indirect(key_list[:]), COPY)
             for g in range(2):
                 cols = slice(g * P, (g + 1) * P)
-                kg = pool.tile([P, P], F32, name=f"kg_half_{t}_{g}")
-                nc.scalar.activation(kg[:], k1[t].indirect(key_list[:, g * HALF_COLS : (g + 1) * HALF_COLS]), COPY)
                 nc.vector.scalar_tensor_tensor(
-                    vk1[g][:, :, t], kg[:], fi_sb[:, 1, t : t + 1], kos[1][t][:, cols], MULT, ADD
+                    early[g][:, t, :], kg[:, cols], fi_sb[:, 1, t : t + 1], kos[1][t][:, cols], MULT, ADD
                 )
-                if t == PACK - 1:
-                    codes, scales = quantise(f"vk_1_{g}", vk1[g], P)
-                    multiply(acc_top[g][:], u1, 0, (codes[:], scales[:]), False, True)
-                    multiply(acc_low[:, cols], u1, 1, (codes[:], scales[:]), False, g == 1)
-
         top = [pool.tile([P, P], F32, name=f"top_{g}") for g in range(2)]
         low = pool.tile([P, I], F32, name="low")
-        for g in range(2):
-            nc.scalar.activation(top[g][:], acc_top[g][:], COPY)
-        nc.vector.tensor_tensor(board[0][:].indirect(col_list[:, 0:HALF_COLS]), top[0][:], bias[:, 0:P], ADD)
-        nc.vector.tensor_tensor(low[:], acc_low[:], bias[:], ADD)
-        nc.vector.tensor_tensor(board[0][:].indirect(col_list[:, HALF_COLS:]), top[1][:], bias[:, P:], ADD)
-        nc.scalar.activation(board[1][:].indirect(col_list[:]), low[:], COPY)
 
-        pieces = [(0, 0, 512), (0, 512, 1024), (1, 0, 512), (1, 512, 768), (1, 768, 1024)]
+        def key_half(t, g, target):
+            kg = pool.tile([P, P], F32, name=f"kg_half_{t}_{g}")
+            nc.scalar.activation(kg[:], k1[t].indirect(key_list[:, g * HALF_COLS : (g + 1) * HALF_COLS]), COPY)
+            nc.vector.scalar_tensor_tensor(
+                target, kg[:], fi_sb[:, 1, t : t + 1], kos[1][t][:, g * P : (g + 1) * P], MULT, ADD
+            )
+
+        def finish_half(g, grouped):
+            codes, scales = quantise(f"vk_1_{g}", grouped, P)
+            multiply(acc_top[g][:], u1, 0, (codes[:], scales[:]), False, True)
+            multiply(acc_low[:, g * P : (g + 1) * P], u1, 1, (codes[:], scales[:]), False, g == 1)
+
+        def place_top(g):
+            nc.vector.tensor_tensor(top[g][:], acc_top[g][:], bias[:, g * P : (g + 1) * P], ADD)
+            nc.scalar.activation(
+                board[0][:].indirect(col_list[:, g * HALF_COLS : (g + 1) * HALF_COLS]), top[g][:], COPY
+            )
+
+        first_half = pool.tile([P, P, PACK], BF16, name="first_half", tag="vk_1", align_bytes=64)
+        key_half(2, 0, early[0][:, 2, :])
+        weave(first_half, early[0][:], 0)
+        key_half(2, 1, early[1][:, 2, :])
+        key_half(3, 0, first_half[:, :, 3])
+        finish_half(0, first_half)
+        key_half(3, 1, early[1][:, 3, :])
+        second_half = pool.tile([P, P, PACK], BF16, name="second_half", tag="vk_1", align_bytes=64)
+        weave(second_half, early[1][:], 0)
+        place_top(0)
+        finish_half(1, second_half)
+        place_top(1)
+        nc.vector.tensor_tensor(low[:], acc_low[:], bias[:], ADD)
+        nc.vector.tensor_copy(board[1][:].indirect(col_list[:, 0:HALF_COLS]), low[:, 0:P])
+        nc.scalar.activation(board[1][:].indirect(col_list[:, HALF_COLS:]), low[:, P:], COPY)
+
+        pieces = [(0, 0, 256), (0, 256, 640), (0, 640, 1024), (1, 0, 512), (1, 512, 832), (1, 832, 1024)]
         for h, lo, hi in pieces:
             best = pool.tile([P, hi - lo], F32, name=f"best_{h}_{lo}")
             nc.vector.tensor_tensor(best[:], board[h][:, lo:hi], old_sb[h][:, lo:hi], MAX)

@@ -3,7 +3,7 @@ from contextlib import ExitStack
 import concourse.mybir as mybir
 from concourse.masks import make_identity
 
-K, T, J, I, V, C = 1024, 1024, 256, 256, 1024, 1024
+K, J, I, C = 1024, 256, 256, 1024
 FLOPS = 2 * K * J * I
 
 F32 = mybir.dt.float32
@@ -20,14 +20,24 @@ COPY = mybir.ActivationFunctionType.Copy
 P = 128
 PACK = 4
 PASSES = K // (P * PACK)
-PAD = 8
+LAST = PACK - 1
 STEP = 0.6
+PAD = 8
 LIST_COLS = J // 16
 HALF_COLS = LIST_COLS // 2
+RUN = 4
+
+FK_ROW, FI_ROW, BI_ROW, SMALL_ROWS = 0, 2, 4, 5
+
+PIECES = [(0, 0, 256), (0, 256, 640), (0, 640, 1024), (1, 0, 512), (1, 512, 832), (1, 832, 1024)]
 
 
-def pass_rows(src, a):
-    return src[a * P * PACK : (a + 1) * P * PACK, :].rearrange("(p t) w -> p t w", t=PACK)
+def half(g):
+    return slice(g * P, (g + 1) * P)
+
+
+def list_half(tile, g):
+    return tile[:, g * HALF_COLS : (g + 1) * HALF_COLS]
 
 
 def tile_list_scores_steps_mixed_placed_f_kernel(tc, xf, fk, kf, ko, fi, bi, old, offs, offs2, offs3, out):
@@ -39,21 +49,21 @@ def tile_list_scores_steps_mixed_placed_f_kernel(tc, xf, fk, kf, ko, fi, bi, old
         tok_list = pool.tile([P, LIST_COLS], U16, name="tok_list")
         key_list = pool.tile([P, LIST_COLS], U16, name="key_list")
         col_list = pool.tile([P, LIST_COLS], U16, name="col_list")
-        fk_sb = pool.tile([P, PASSES, PAD], F32, name="fk_sb")
-        fi_sb = pool.tile([P, PASSES, PAD], F32, name="fi_sb")
-        bi_sb = pool.tile([P, 2], F32, name="bi_sb")
+        rows_in = pool.tile([P, P * PACK], F32, name="rows_in")
+        nc.vector.memset(rows_in[:], 0.0)
         ko_sb = pool.tile([P, PASSES, PACK * I], F32, name="ko_sb")
         old_sb = [pool.tile([P, C], F32, name=f"old_{h}") for h in range(2)]
 
         def load_planes(name, src, a, first, count):
             planes = pool.tile([P, count, src.shape[1]], F32, name=f"{name}_{a}_{first}")
-            nc.sync.dma_start(planes[:], pass_rows(src, a)[:, first : first + count, :])
+            rows = src[a * P * PACK : (a + 1) * P * PACK, :].rearrange("(p t) w -> p t w", t=PACK)
+            nc.sync.dma_start(planes[:], rows[:, first : first + count, :])
             return [planes[:, e, :] for e in range(count)]
 
-        nc.scalar.dma_start(fi_sb[:, :, 0:PACK], fi.rearrange("(a p t) o -> p a (t o)", a=PASSES, t=PACK))
         nc.sync.dma_start(ko_sb[:], ko.rearrange("(a p t) i -> p a (t i)", a=PASSES, t=PACK))
-        nc.scalar.dma_start(fk_sb[:, :, 0:PACK], fk.rearrange("(a p t) o -> p a (t o)", a=PASSES, t=PACK))
-        nc.scalar.dma_start(bi_sb[:], bi.rearrange("o (p m) -> p (o m)", m=2))
+        nc.sync.dma_start(rows_in[FK_ROW : FK_ROW + PASSES, :], fk.rearrange("(a k) o -> a (k o)", a=PASSES))
+        nc.sync.dma_start(rows_in[FI_ROW : FI_ROW + PASSES, :], fi.rearrange("(a k) o -> a (k o)", a=PASSES))
+        nc.sync.dma_start(rows_in[BI_ROW : BI_ROW + 1, 0:I], bi)
         nc.sync.dma_start(tok_list[:], offs)
         x0 = load_planes("x", xf, 0, 0, PACK)
         nc.sync.dma_start(key_list[:], offs2)
@@ -62,44 +72,68 @@ def tile_list_scores_steps_mixed_placed_f_kernel(tc, xf, fk, kf, ko, fi, bi, old
         k1 = [load_planes("k", kf, 1, t, 1)[0] for t in range(PACK)]
         nc.sync.dma_start(col_list[:], offs3)
         for h in range(2):
-            nc.sync.dma_start(old_sb[h][:], old[h * P : (h + 1) * P, :])
+            nc.sync.dma_start(old_sb[h][:], old[half(h), :])
 
-        zeros = pool.tile([P, PAD], F32, name="zeros")
-        nc.gpsimd.memset(zeros[:], 0.0)
+        zero = pool.tile([P, 1], F32, name="zero")
+        nc.gpsimd.memset(zero[:], 0.0)
         ident = pool.tile([P, P], F32, name="ident")
         make_identity(nc, ident[:])
         xg = [[pool.tile([P, PAD + J], F32, name=f"xg_{a}_{t}") for t in range(PACK)] for a in range(PASSES)]
         for a in range(PASSES):
             for t in range(PACK):
-                nc.scalar.activation(xg[a][t][:, 0:PAD], zeros[:], COPY)
+                nc.scalar.activation(xg[a][t][:, PAD - 1 : PAD], zero[:], COPY)
         board = [pool.tile([P, C], F32, name=f"board_{h}") for h in range(2)]
         for h in range(2):
             nc.gpsimd.memset(board[h][:], 0.0)
 
-        bias_ps = psum.tile([P, 2, P], F32, name="bias_ps")
-        for m in range(2):
-            nc.tensor.transpose(bias_ps[:, m, :], bi_sb[:, m : m + 1].to_broadcast([P, P]), ident[:])
+        turned = psum.tile([P, PACK, P], F32, name="turned")
+        for t in range(PACK):
+            nc.tensor.transpose(turned[:, t, :], rows_in[:, t::PACK], ident[:])
+        small = pool.tile([P, PACK, SMALL_ROWS], F32, name="small")
+        nc.scalar.activation(small[:], turned[:, :, 0:SMALL_ROWS], COPY)
+
+        def factor(row, a, t):
+            return small[:, t, row + a : row + a + 1]
+
+        spread = psum.tile([P, PACK, P], F32, name="spread")
+        for t in range(PACK):
+            nc.tensor.transpose(spread[:, t, :], small[:, t, BI_ROW : BI_ROW + 1].to_broadcast([P, P]), ident[:])
         bias = pool.tile([P, I], F32, name="bias")
-        nc.scalar.activation(bias[:].rearrange("p (n m) -> p n m", m=2), bias_ps[:].rearrange("p m n -> p n m"), COPY)
+        nc.scalar.activation(
+            bias[:].rearrange("p (n t) -> p n t", t=PACK),
+            spread[:, :, 0 : I // PACK].rearrange("p t n -> p n t"),
+            COPY,
+        )
 
-        def quantise(name, grouped, width):
-            codes = pool.tile([P, width], U32, name=name + "_codes", align_bytes=64)
-            scales = pool.tile([P, width], U8, name=name + "_scales", align_bytes=64)
-            nc.vector.quantize_mx(codes[:].bitcast(E5M2X4), scales[:], grouped[:].rearrange("p w t -> p (w t)"))
-            return codes, scales
-
-        kos = [[pool.tile([P, I], F32, name=f"kos_{a}_{t}") for t in range(PACK)] for a in range(PASSES)]
+        ko_fi = [[pool.tile([P, I], F32, name=f"ko_fi_{a}_{t}") for t in range(PACK)] for a in range(PASSES)]
         for a in range(PASSES):
             for t in range(PACK):
                 nc.gpsimd.tensor_scalar(
-                    kos[a][t][:], ko_sb[:, a, t * I : (t + 1) * I], fi_sb[:, a, t : t + 1], 0.0, MULT, ADD
+                    ko_fi[a][t][:], ko_sb[:, a, t * I : (t + 1) * I], factor(FI_ROW, a, t), 0.0, MULT, ADD
                 )
 
-        def weave(grouped, planes, first):
+        def weave(woven, planes, first):
             count = planes.shape[1]
             nc.vector.tensor_copy(
-                grouped[:, :, first : first + count].rearrange("p (c i) e -> p c e i", i=4),
-                planes.rearrange("p e (c i) -> p c e i", i=4),
+                woven[:, :, first : first + count].rearrange("p (c i) e -> p c e i", i=RUN),
+                planes.rearrange("p e (c i) -> p c e i", i=RUN),
+            )
+
+        def quantise(name, woven, width):
+            codes = pool.tile([P, width], U32, name=name + "_codes", align_bytes=64)
+            scales = pool.tile([P, width], U8, name=name + "_scales", align_bytes=64)
+            nc.vector.quantize_mx(codes[:].bitcast(E5M2X4), scales[:], woven[:].rearrange("p w t -> p (w t)"))
+            return codes, scales
+
+        def multiply(acc, u, h, vk, cols, start, stop):
+            nc.tensor.matmul_mx(
+                acc,
+                u[0][:, half(h)].bitcast(E5M2X4),
+                u[1][:, half(h)],
+                vk[0][:, cols].bitcast(E5M2X4),
+                vk[1][:, cols],
+                start=start,
+                stop=stop,
             )
 
         def token_planes(a, first, count, windows):
@@ -111,89 +145,78 @@ def tile_list_scores_steps_mixed_placed_f_kernel(tc, xf, fk, kf, ko, fi, bi, old
                 nc.vector.scalar_tensor_tensor(
                     diff[:], xg[a][t][:, PAD - 1 : PAD - 1 + J], -STEP, xg[a][t][:, PAD:], MULT, ADD
                 )
-                nc.vector.tensor_scalar(planes[:, e, :], diff[:], fk_sb[:, a, t : t + 1], None, MULT)
+                nc.vector.tensor_scalar(planes[:, e, :], diff[:], factor(FK_ROW, a, t), None, MULT)
             return planes
 
-        def key_planes(a, first, count, windows):
-            planes = pool.tile([P, count, I], BF16, name=f"vk_planes_{a}_{first}")
-            for e in range(count):
-                t = first + e
-                kg = pool.tile([P, I], F32, name=f"kg_{a}_{t}")
-                nc.scalar.activation(kg[:], windows[t].indirect(key_list[:]), COPY)
-                nc.vector.scalar_tensor_tensor(planes[:, e, :], kg[:], fi_sb[:, a, t : t + 1], kos[a][t][:], MULT, ADD)
-            return planes
+        def gather_keys(name, window, offsets, width):
+            picked = pool.tile([P, width], F32, name=name)
+            nc.scalar.activation(picked[:], window.indirect(offsets), COPY)
+            return picked
 
-        def multiply(acc, u, h, v, start, stop):
-            rows = slice(h * P, (h + 1) * P)
-            nc.tensor.matmul_mx(
-                acc, u[0][:, rows].bitcast(E5M2X4), u[1][:, rows], v[0].bitcast(E5M2X4), v[1], start=start, stop=stop
-            )
+        def combine_keys(target, picked, a, t, cols):
+            nc.vector.scalar_tensor_tensor(target, picked, factor(FI_ROW, a, t), ko_fi[a][t][:, cols], MULT, ADD)
 
-        ug0 = pool.tile([P, J, PACK], BF16, name="u_0", align_bytes=64)
-        weave(ug0, token_planes(0, 0, PACK, x0)[:], 0)
-        u0 = quantise("u_0", ug0, J)
-        vk0 = pool.tile([P, I, PACK], BF16, name="vk_0", align_bytes=64)
-        weave(vk0, key_planes(0, 0, PACK, k0)[:], 0)
-        v0 = quantise("vk_0", vk0, I)
+        whole = slice(0, I)
+
+        u_woven0 = pool.tile([P, J, PACK], BF16, name="u_woven0", align_bytes=64)
+        weave(u_woven0, token_planes(0, 0, PACK, x0)[:], 0)
+        u0 = quantise("u_0", u_woven0, J)
+        vk_planes0 = pool.tile([P, PACK, I], BF16, name="vk_planes0")
+        for t in range(PACK):
+            combine_keys(vk_planes0[:, t, :], gather_keys(f"kg_0_{t}", k0[t], key_list[:], I)[:], 0, t, whole)
+        vk_woven0 = pool.tile([P, I, PACK], BF16, name="vk_woven0", align_bytes=64)
+        weave(vk_woven0, vk_planes0[:], 0)
+        vk0 = quantise("vk_0", vk_woven0, I)
         acc_top = [psum.tile([P, P], F32, name=f"acc_top_{g}") for g in range(2)]
         acc_low = psum.tile([P, I], F32, name="acc_low")
         for g in range(2):
-            cols = slice(g * P, (g + 1) * P)
-            multiply(acc_top[g][:], u0, 0, (v0[0][:, cols], v0[1][:, cols]), True, False)
-        multiply(acc_low[:], u0, 1, (v0[0][:], v0[1][:]), True, False)
+            multiply(acc_top[g][:], u0, 0, vk0, half(g), True, False)
+        multiply(acc_low[:], u0, 1, vk0, whole, True, False)
 
-        ug1 = pool.tile([P, J, PACK], BF16, name="u_1", align_bytes=64)
+        u_woven1 = pool.tile([P, J, PACK], BF16, name="u_woven1", align_bytes=64)
         for first in (0, 2):
-            weave(ug1, token_planes(1, first, 2, x1)[:], first)
-        u1 = quantise("u_1", ug1, J)
-        early = [pool.tile([P, PACK - 1 + g, P], BF16, name=f"early_{g}") for g in range(2)]
+            weave(u_woven1, token_planes(1, first, 2, x1)[:], first)
+        u1 = quantise("u_1", u_woven1, J)
+
+        vk_planes1 = [pool.tile([P, LAST + g, P], BF16, name=f"vk_planes1_{g}") for g in range(2)]
         for t in range(2):
-            kg = pool.tile([P, I], F32, name=f"kg_1_{t}")
-            nc.scalar.activation(kg[:], k1[t].indirect(key_list[:]), COPY)
+            picked = gather_keys(f"kg_1_{t}", k1[t], key_list[:], I)
             for g in range(2):
-                cols = slice(g * P, (g + 1) * P)
-                nc.vector.scalar_tensor_tensor(
-                    early[g][:, t, :], kg[:, cols], fi_sb[:, 1, t : t + 1], kos[1][t][:, cols], MULT, ADD
-                )
+                combine_keys(vk_planes1[g][:, t, :], picked[:, half(g)], 1, t, half(g))
         top = [pool.tile([P, P], F32, name=f"top_{g}") for g in range(2)]
         low = pool.tile([P, I], F32, name="low")
 
         def key_half(t, g, target):
-            kg = pool.tile([P, P], F32, name=f"kg_half_{t}_{g}")
-            nc.scalar.activation(kg[:], k1[t].indirect(key_list[:, g * HALF_COLS : (g + 1) * HALF_COLS]), COPY)
-            nc.vector.scalar_tensor_tensor(
-                target, kg[:], fi_sb[:, 1, t : t + 1], kos[1][t][:, g * P : (g + 1) * P], MULT, ADD
-            )
+            picked = gather_keys(f"kg_half_{t}_{g}", k1[t], list_half(key_list, g), P)
+            combine_keys(target, picked[:], 1, t, half(g))
 
-        def finish_half(g, grouped):
-            codes, scales = quantise(f"vk_1_{g}", grouped, P)
-            multiply(acc_top[g][:], u1, 0, (codes[:], scales[:]), False, True)
-            multiply(acc_low[:, g * P : (g + 1) * P], u1, 1, (codes[:], scales[:]), False, g == 1)
+        def finish_half(g, woven):
+            vk1 = quantise(f"vk_1_{g}", woven, P)
+            multiply(acc_top[g][:], u1, 0, vk1, half(0), False, True)
+            multiply(acc_low[:, half(g)], u1, 1, vk1, half(0), False, g == 1)
 
         def place_top(g):
-            nc.vector.tensor_tensor(top[g][:], acc_top[g][:], bias[:, g * P : (g + 1) * P], ADD)
-            nc.scalar.activation(
-                board[0][:].indirect(col_list[:, g * HALF_COLS : (g + 1) * HALF_COLS]), top[g][:], COPY
-            )
+            nc.vector.tensor_tensor(top[g][:], acc_top[g][:], bias[:, half(g)], ADD)
+            nc.scalar.activation(board[0][:].indirect(list_half(col_list, g)), top[g][:], COPY)
 
-        first_half = pool.tile([P, P, PACK], BF16, name="first_half", tag="vk_1", align_bytes=64)
-        key_half(2, 0, early[0][:, 2, :])
-        weave(first_half, early[0][:], 0)
-        key_half(2, 1, early[1][:, 2, :])
-        key_half(3, 0, first_half[:, :, 3])
+        first_half = pool.tile([P, P, PACK], BF16, name="first_half", tag="vk_woven1", align_bytes=64)
+        key_half(2, 0, vk_planes1[0][:, 2, :])
+        weave(first_half, vk_planes1[0][:], 0)
+        key_half(2, 1, vk_planes1[1][:, 2, :])
+        key_half(LAST, 0, first_half[:, :, LAST])
         finish_half(0, first_half)
-        key_half(3, 1, early[1][:, 3, :])
-        second_half = pool.tile([P, P, PACK], BF16, name="second_half", tag="vk_1", align_bytes=64)
-        weave(second_half, early[1][:], 0)
+        key_half(LAST, 1, vk_planes1[1][:, LAST, :])
+        second_half = pool.tile([P, P, PACK], BF16, name="second_half", tag="vk_woven1", align_bytes=64)
+        weave(second_half, vk_planes1[1][:], 0)
         place_top(0)
         finish_half(1, second_half)
         place_top(1)
-        nc.vector.tensor_tensor(low[:], acc_low[:], bias[:], ADD)
-        nc.vector.tensor_copy(board[1][:].indirect(col_list[:, 0:HALF_COLS]), low[:, 0:P])
-        nc.scalar.activation(board[1][:].indirect(col_list[:, HALF_COLS:]), low[:, P:], COPY)
 
-        pieces = [(0, 0, 256), (0, 256, 640), (0, 640, 1024), (1, 0, 512), (1, 512, 832), (1, 832, 1024)]
-        for h, lo, hi in pieces:
+        nc.vector.tensor_tensor(low[:], acc_low[:], bias[:], ADD)
+        nc.vector.tensor_copy(board[1][:].indirect(list_half(col_list, 0)), low[:, half(0)])
+        nc.scalar.activation(board[1][:].indirect(list_half(col_list, 1)), low[:, half(1)], COPY)
+
+        for h, lo, hi in PIECES:
             best = pool.tile([P, hi - lo], F32, name=f"best_{h}_{lo}")
             nc.vector.tensor_tensor(best[:], board[h][:, lo:hi], old_sb[h][:, lo:hi], MAX)
-            nc.sync.dma_start(out[h * P : (h + 1) * P, lo:hi], best[:])
+            nc.sync.dma_start(out[half(h), lo:hi], best[:])

from contextlib import ExitStack

import concourse.mybir as mybir
from concourse.masks import make_identity

K, J, I, C = 1024, 256, 256, 1024
FLOPS = 2 * K * J * I

F32 = mybir.dt.float32
BF16 = mybir.dt.bfloat16
U32 = mybir.dt.uint32
U16 = mybir.dt.uint16
U8 = mybir.dt.uint8
E5M2X4 = mybir.dt.float8_e5m2_x4
MULT = mybir.AluOpType.mult
ADD = mybir.AluOpType.add
MAX = mybir.AluOpType.max
COPY = mybir.ActivationFunctionType.Copy

P = 128
PACK = 4
PASSES = K // (P * PACK)
LAST = PACK - 1
STEP = 0.6
PAD = 8
LIST_COLS = J // 16
HALF_COLS = LIST_COLS // 2
RUN = 4

FK_ROW, FI_ROW, BI_ROW, SMALL_ROWS = 0, 2, 4, 5

PIECES = [(0, 0, 256), (0, 256, 640), (0, 640, 1024), (1, 0, 512), (1, 512, 832), (1, 832, 1024)]


def half(g):
    return slice(g * P, (g + 1) * P)


def list_half(tile, g):
    return tile[:, g * HALF_COLS : (g + 1) * HALF_COLS]


def tile_list_scores_steps_mixed_placed_f_kernel(tc, xf, fk, kf, ko, fi, bi, old, offs, offs2, offs3, out):
    nc = tc.nc
    with ExitStack() as ctx:
        pool = ctx.enter_context(tc.tile_pool(name="pool", bufs=1))
        psum = ctx.enter_context(tc.psum_pool(name="psum", bufs=1))

        tok_list = pool.tile([P, LIST_COLS], U16, name="tok_list")
        key_list = pool.tile([P, LIST_COLS], U16, name="key_list")
        col_list = pool.tile([P, LIST_COLS], U16, name="col_list")
        rows_in = pool.tile([P, P * PACK], F32, name="rows_in")
        nc.vector.memset(rows_in[:], 0.0)
        ko_sb = pool.tile([P, PASSES, PACK * I], F32, name="ko_sb")
        old_sb = [pool.tile([P, C], F32, name=f"old_{h}") for h in range(2)]

        def load_planes(name, src, a, first, count):
            planes = pool.tile([P, count, src.shape[1]], F32, name=f"{name}_{a}_{first}")
            rows = src[a * P * PACK : (a + 1) * P * PACK, :].rearrange("(p t) w -> p t w", t=PACK)
            nc.sync.dma_start(planes[:], rows[:, first : first + count, :])
            return [planes[:, e, :] for e in range(count)]

        nc.sync.dma_start(ko_sb[:], ko.rearrange("(a p t) i -> p a (t i)", a=PASSES, t=PACK))
        nc.sync.dma_start(rows_in[FK_ROW : FK_ROW + PASSES, :], fk.rearrange("(a k) o -> a (k o)", a=PASSES))
        nc.sync.dma_start(rows_in[FI_ROW : FI_ROW + PASSES, :], fi.rearrange("(a k) o -> a (k o)", a=PASSES))
        nc.sync.dma_start(rows_in[BI_ROW : BI_ROW + 1, 0:I], bi)
        nc.sync.dma_start(tok_list[:], offs)
        x0 = load_planes("x", xf, 0, 0, PACK)
        nc.sync.dma_start(key_list[:], offs2)
        k0 = load_planes("k", kf, 0, 0, 2) + load_planes("k", kf, 0, 2, 2)
        x1 = load_planes("x", xf, 1, 0, 2) + load_planes("x", xf, 1, 2, 1) + load_planes("x", xf, 1, 3, 1)
        k1 = [load_planes("k", kf, 1, t, 1)[0] for t in range(PACK)]
        nc.sync.dma_start(col_list[:], offs3)
        for h in range(2):
            nc.sync.dma_start(old_sb[h][:], old[half(h), :])

        zero = pool.tile([P, 1], F32, name="zero")
        nc.gpsimd.memset(zero[:], 0.0)
        ident = pool.tile([P, P], F32, name="ident")
        make_identity(nc, ident[:])
        xg = [[pool.tile([P, PAD + J], F32, name=f"xg_{a}_{t}") for t in range(PACK)] for a in range(PASSES)]
        for a in range(PASSES):
            for t in range(PACK):
                nc.scalar.activation(xg[a][t][:, PAD - 1 : PAD], zero[:], COPY)
        board = [pool.tile([P, C], F32, name=f"board_{h}") for h in range(2)]
        for h in range(2):
            nc.gpsimd.memset(board[h][:], 0.0)

        turned = psum.tile([P, PACK, P], F32, name="turned")
        for t in range(PACK):
            nc.tensor.transpose(turned[:, t, :], rows_in[:, t::PACK], ident[:])
        small = pool.tile([P, PACK, SMALL_ROWS], F32, name="small")
        nc.scalar.activation(small[:], turned[:, :, 0:SMALL_ROWS], COPY)

        def factor(row, a, t):
            return small[:, t, row + a : row + a + 1]

        spread = psum.tile([P, PACK, P], F32, name="spread")
        for t in range(PACK):
            nc.tensor.transpose(spread[:, t, :], small[:, t, BI_ROW : BI_ROW + 1].to_broadcast([P, P]), ident[:])
        bias = pool.tile([P, I], F32, name="bias")
        nc.scalar.activation(
            bias[:].rearrange("p (n t) -> p n t", t=PACK),
            spread[:, :, 0 : I // PACK].rearrange("p t n -> p n t"),
            COPY,
        )

        ko_fi = [[pool.tile([P, I], F32, name=f"ko_fi_{a}_{t}") for t in range(PACK)] for a in range(PASSES)]
        for a in range(PASSES):
            for t in range(PACK):
                nc.gpsimd.tensor_scalar(
                    ko_fi[a][t][:], ko_sb[:, a, t * I : (t + 1) * I], factor(FI_ROW, a, t), 0.0, MULT, ADD
                )

        def weave(woven, planes, first):
            count = planes.shape[1]
            nc.vector.tensor_copy(
                woven[:, :, first : first + count].rearrange("p (c i) e -> p c e i", i=RUN),
                planes.rearrange("p e (c i) -> p c e i", i=RUN),
            )

        def quantise(name, woven, width):
            codes = pool.tile([P, width], U32, name=name + "_codes", align_bytes=64)
            scales = pool.tile([P, width], U8, name=name + "_scales", align_bytes=64)
            nc.vector.quantize_mx(codes[:].bitcast(E5M2X4), scales[:], woven[:].rearrange("p w t -> p (w t)"))
            return codes, scales

        def multiply(acc, u, h, vk, cols, start, stop):
            nc.tensor.matmul_mx(
                acc,
                u[0][:, half(h)].bitcast(E5M2X4),
                u[1][:, half(h)],
                vk[0][:, cols].bitcast(E5M2X4),
                vk[1][:, cols],
                start=start,
                stop=stop,
            )

        def token_planes(a, first, count, windows):
            planes = pool.tile([P, count, J], BF16, name=f"u_planes_{a}_{first}")
            for e in range(count):
                t = first + e
                nc.scalar.activation(xg[a][t][:, PAD:], windows[t].indirect(tok_list[:]), COPY)
                diff = pool.tile([P, J], F32, name=f"diff_{a}_{t}")
                nc.vector.scalar_tensor_tensor(
                    diff[:], xg[a][t][:, PAD - 1 : PAD - 1 + J], -STEP, xg[a][t][:, PAD:], MULT, ADD
                )
                nc.vector.tensor_scalar(planes[:, e, :], diff[:], factor(FK_ROW, a, t), None, MULT)
            return planes

        def gather_keys(name, window, offsets, width):
            picked = pool.tile([P, width], F32, name=name)
            nc.scalar.activation(picked[:], window.indirect(offsets), COPY)
            return picked

        def combine_keys(target, picked, a, t, cols):
            nc.vector.scalar_tensor_tensor(target, picked, factor(FI_ROW, a, t), ko_fi[a][t][:, cols], MULT, ADD)

        whole = slice(0, I)

        u_woven0 = pool.tile([P, J, PACK], BF16, name="u_woven0", align_bytes=64)
        weave(u_woven0, token_planes(0, 0, PACK, x0)[:], 0)
        u0 = quantise("u_0", u_woven0, J)
        vk_planes0 = pool.tile([P, PACK, I], BF16, name="vk_planes0")
        for t in range(PACK):
            combine_keys(vk_planes0[:, t, :], gather_keys(f"kg_0_{t}", k0[t], key_list[:], I)[:], 0, t, whole)
        vk_woven0 = pool.tile([P, I, PACK], BF16, name="vk_woven0", align_bytes=64)
        weave(vk_woven0, vk_planes0[:], 0)
        vk0 = quantise("vk_0", vk_woven0, I)
        acc_top = [psum.tile([P, P], F32, name=f"acc_top_{g}") for g in range(2)]
        acc_low = psum.tile([P, I], F32, name="acc_low")
        for g in range(2):
            multiply(acc_top[g][:], u0, 0, vk0, half(g), True, False)
        multiply(acc_low[:], u0, 1, vk0, whole, True, False)

        u_woven1 = pool.tile([P, J, PACK], BF16, name="u_woven1", align_bytes=64)
        for first in (0, 2):
            weave(u_woven1, token_planes(1, first, 2, x1)[:], first)
        u1 = quantise("u_1", u_woven1, J)

        vk_planes1 = [pool.tile([P, LAST + g, P], BF16, name=f"vk_planes1_{g}") for g in range(2)]
        for t in range(2):
            picked = gather_keys(f"kg_1_{t}", k1[t], key_list[:], I)
            for g in range(2):
                combine_keys(vk_planes1[g][:, t, :], picked[:, half(g)], 1, t, half(g))
        top = [pool.tile([P, P], F32, name=f"top_{g}") for g in range(2)]
        low = pool.tile([P, I], F32, name="low")

        def key_half(t, g, target):
            picked = gather_keys(f"kg_half_{t}_{g}", k1[t], list_half(key_list, g), P)
            combine_keys(target, picked[:], 1, t, half(g))

        def finish_half(g, woven):
            vk1 = quantise(f"vk_1_{g}", woven, P)
            multiply(acc_top[g][:], u1, 0, vk1, half(0), False, True)
            multiply(acc_low[:, half(g)], u1, 1, vk1, half(0), False, g == 1)

        def place_top(g):
            nc.vector.tensor_tensor(top[g][:], acc_top[g][:], bias[:, half(g)], ADD)
            nc.scalar.activation(board[0][:].indirect(list_half(col_list, g)), top[g][:], COPY)

        first_half = pool.tile([P, P, PACK], BF16, name="first_half", tag="vk_woven1", align_bytes=64)
        key_half(2, 0, vk_planes1[0][:, 2, :])
        weave(first_half, vk_planes1[0][:], 0)
        key_half(2, 1, vk_planes1[1][:, 2, :])
        key_half(LAST, 0, first_half[:, :, LAST])
        finish_half(0, first_half)
        key_half(LAST, 1, vk_planes1[1][:, LAST, :])
        second_half = pool.tile([P, P, PACK], BF16, name="second_half", tag="vk_woven1", align_bytes=64)
        weave(second_half, vk_planes1[1][:], 0)
        place_top(0)
        finish_half(1, second_half)
        place_top(1)

        nc.vector.tensor_tensor(low[:], acc_low[:], bias[:], ADD)
        nc.vector.tensor_copy(board[1][:].indirect(list_half(col_list, 0)), low[:, half(0)])
        nc.scalar.activation(board[1][:].indirect(list_half(col_list, 1)), low[:, half(1)], COPY)

        for h, lo, hi in PIECES:
            best = pool.tile([P, hi - lo], F32, name=f"best_{h}_{lo}")
            nc.vector.tensor_tensor(best[:], board[h][:, lo:hi], old_sb[h][:, lo:hi], MAX)
            nc.sync.dma_start(out[half(h), lo:hi], best[:])
